import numpy as np
import ml_dtypes


def mxq(x, axis, fmt="e4m3"):
    dtype, down = {"e4m3": (ml_dtypes.float8_e4m3fn, 7), "e5m2": (ml_dtypes.float8_e5m2, 14)}[fmt]
    v = np.moveaxis(np.asarray(x, np.float32).astype(ml_dtypes.bfloat16).astype(np.float64), axis, -1)
    blocks = v.reshape(v.shape[:-1] + (-1, 32))
    amax = np.abs(blocks).max(-1, keepdims=True)
    byte = np.maximum(np.where(amax > 0, np.frexp(amax)[1] - 1 + 127, 0) - down, 1)
    scale = np.exp2(byte - 127.0)
    codes = (blocks / scale).astype(np.float32).astype(dtype).astype(np.float64)
    return np.moveaxis((codes * scale).reshape(v.shape), -1, axis)


WIDE = False


def mx_kscale(k):
    if not WIDE:
        return np.ones(k)
    levels = np.array([10, -10, 5, -5, 0])
    if k % 512:
        return np.exp2(np.random.permutation(np.resize(levels, k // 32))).repeat(32)
    a = np.empty((k // 512, 16))
    for p in range(k // 512):
        a[p, :8] = np.random.permutation(np.resize(levels, 8))
        for g in range(8):
            far = levels[np.abs(levels - a[p, g]) >= 10]
            a[p, g + 8] = far[np.random.randint(len(far))]
    return np.exp2(a.ravel()).repeat(32)


def f64(x):
    return np.asarray(x).astype(np.float64)


def striped(idx):
    return np.tile(idx.reshape(-1, 16).T, (8, 1)).astype(np.uint16)


def unstriped(offs):
    return offs[:16].T.reshape(-1).astype(np.int64)


def pack_weight(w):
    k, n = w.shape
    w = f64(np.asarray(w, np.float32).astype(ml_dtypes.bfloat16)).reshape(k // 32, 32, n)
    amax = np.abs(w).max(1)
    byte = np.clip(np.where(amax > 0, np.frexp(amax)[1] - 1 + 127 - 7, 1), 1, 254)
    scaled = (w * np.exp2(127.0 - byte)[:, None, :]).reshape(k, n).astype(np.float32)
    words = np.ascontiguousarray(scaled.reshape(k // 512, 128, 4, n).transpose(0, 1, 3, 2)).astype(ml_dtypes.float8_e4m3fn).view(np.uint8)
    return words, np.ascontiguousarray(byte.astype(np.uint8).reshape(k // 512, 16, n))


def unpack_weight(words, scales):
    g, p, n, _ = words.shape
    vals = np.ascontiguousarray(words).view(ml_dtypes.float8_e4m3fn).astype(np.float64) * np.repeat(np.exp2(scales.astype(np.float64) - 127.0), 8, axis=1)[..., None]
    return vals.transpose(0, 1, 3, 2).reshape(g * 512, n)


K, T, S, D, R, G = 1024, 1024, 512, 32, 256, 8
P = 2 ** 7


def setup_inputs():
    n = np.random.standard_normal
    s = mx_kscale(K)[:, None]
    perm = (np.random.permutation(D)[:, None] + D * np.arange(G)[None, :]).reshape(-1)
    packed_xT = pack_weight(n((K, T)) * s)
    return {
        "x_words": packed_xT[0],
        "x_scales": packed_xT[1],
        "fm": (n((K, R)) / np.sqrt(K) / s).astype(np.float32),
        "meas": (n((S, R))).astype(np.float32),
        "prec": (np.tile(np.random.uniform(0.05, 0.2, R), (P, 1))).astype(np.float32),
        "prior": (np.tile(0.5 * n(G), (P, 1))).astype(np.float32),
        "gain": (np.tile(np.random.uniform(0.2, 0.8, R), (P, 1))).astype(np.float32),
        "offs": striped(np.random.permutation(T)[:S]),
        "byf": striped(perm),
    }


def reference(x_words, x_scales, fm, meas, prec, prior, gain, offs, byf):
    xq = unpack_weight(x_words, x_scales)[:, unstriped(offs)]
    fmq = mxq(f64(fm), 0, "e4m3")
    y = xq.T @ fmq
    dd = f64(meas) - y
    d2 = ((dd) ** 2) * f64(prec)[:1]
    lm = f64(prior)[:1] - (0.5 * (d2.reshape(len(d2), -1, D).sum(axis=2)))
    ex = np.exp(lm - lm.max(axis=1, keepdims=True))
    mu = ex / ex.sum(axis=1, keepdims=True)
    ww = np.repeat(mu, D, axis=1) * (y + dd * f64(gain)[:1])
    wf = ww[:, unstriped(byf)]
    return wf.reshape(len(wf), -1, 8).sum(axis=2)

@@ -1,0 +1,245 @@
+from contextlib import ExitStack
+
+import concourse.mybir as mybir
+from concourse.masks import make_identity
+
+K, T, S, R, G, D = 1024, 1024, 512, 256, 8, 32
+FLOPS = 2 * K * S * R
+
+F32 = mybir.dt.float32
+BF16 = mybir.dt.bfloat16
+I32 = mybir.dt.int32
+U32 = mybir.dt.uint32
+U16 = mybir.dt.uint16
+U8 = mybir.dt.uint8
+FP8X4 = mybir.dt.float8_e4m3fn_x4
+ALU = mybir.AluOpType
+ACT = mybir.ActivationFunctionType
+AXIS_X = mybir.AxisListType.X
+
+P = 128
+PACK = 4
+PASSES = K // (P * PACK)
+BLOCKS = R // P
+HALVES = 2
+HALF = S // HALVES
+TILES = HALF // P
+RUN = D // BLOCKS
+WINDOW = 352
+PITCH = RUN + 2
+
+
+def tile_picked_yimm_mean_p_kernel(
+    tc, x_words, x_scales, fm, meas, prec, prior, gain, offs, byf, out
+):
+    nc = tc.nc
+    with ExitStack() as ctx:
+        sb = ctx.enter_context(tc.tile_pool(name="sb", bufs=1))
+        ps = ctx.enter_context(tc.psum_pool(name="ps", bufs=1))
+
+        def sbuf(name, shape, dtype=F32):
+            return sb.tile(shape, dtype, name=name, align_bytes=64)
+
+        def bank(tag, name):
+            return ps.tile([P, 512], F32, name=name, tag=tag)
+
+        def transpose_into(dst, src, first, last):
+            nc.tensor.matmul(dst, src, ident[:], start=first, stop=last, is_transpose=True)
+
+        picks = sb.tile([P, S // 16], U16, name="picks")
+        by_feature = sb.tile([P, R // 16], U16, name="by_feature")
+        words = [sbuf("words%d" % o, [P, T], I32) for o in range(PASSES)]
+        planes = sbuf("planes", [P, T], U8)
+        fm_rows = [sbuf("fm_rows%d" % o, [P, PACK, R]) for o in range(PASSES)]
+        meas_rows = [sbuf("meas_rows%d" % h, [P, TILES, R]) for h in range(HALVES)]
+        prec_col = sbuf("prec_col", [P, BLOCKS])
+        gain_col = sbuf("gain_col", [P, BLOCKS])
+        prior_row = sbuf("prior_row", [P, G])
+        windows = [sbuf("window%d" % n, [P, WINDOW]) for n in range(HALVES * TILES)]
+        ident = sbuf("ident", [P, P])
+        warm = sbuf("warm", [P, 1])
+        warm_out = sbuf("warm_out", [P, 1])
+
+        nc.vector.memset(planes[:].bitcast(I32), 0)
+        nc.vector.memset(warm[:], 0.0)
+        nc.scalar.activation(warm_out[:], warm[:], ACT.Exp)
+        make_identity(nc, ident[:])
+        for window in windows:
+            nc.vector.memset(window[:, R:], 0.0)
+
+        def load_words(o):
+            nc.sync.dma_start(words[o][:], x_words[o].rearrange("p n t -> p (n t)").bitcast(I32))
+
+        def load_fm(o):
+            rows = fm[o * P * PACK : (o + 1) * P * PACK, :]
+            nc.sync.dma_start(fm_rows[o][:], rows.rearrange("(p t) e -> p t e", t=PACK))
+
+        def load_meas(h):
+            rows = meas[h * HALF : (h + 1) * HALF, :]
+            nc.sync.dma_start(meas_rows[h][:], rows.rearrange("(i p) e -> p i e", p=P))
+
+        def load_planes():
+            for q in range(4):
+                nc.sync.dma_start(
+                    planes[32 * q : 32 * q + 4 * PASSES, :].bitcast(I32),
+                    x_scales[:, 4 * q : 4 * q + 4, :].bitcast(I32),
+                )
+
+        nc.sync.dma_start(picks[:], offs)
+        nc.sync.dma_start(prior_row[:], prior)
+        load_words(0)
+        load_planes()
+        load_fm(0)
+        load_meas(0)
+        load_meas(1)
+        load_fm(1)
+        nc.sync.dma_start(prec_col[:], prec[0, :].rearrange("(p b) -> p b", b=BLOCKS))
+        nc.sync.dma_start(gain_col[:], gain[0, :].rearrange("(p b) -> p b", b=BLOCKS))
+        load_words(1)
+        nc.sync.dma_start(by_feature[:], byf)
+
+        picked_words = [sbuf("picked_words%d" % o, [P, S], U32) for o in range(PASSES)]
+        picked_planes = sbuf("picked_planes", [P, S], U8)
+        fm_codes = {}
+        fm_planes = {}
+        y_bank = {}
+        meas_t = {}
+        update_bank = {}
+        misfit_bank = {}
+
+        def gather_words(o, lo, hi):
+            nc.vector.tensor_copy(
+                picked_words[o][:, lo:hi], words[o][:].bitcast(U32).indirect(picks[:, lo // 16 : hi // 16])
+            )
+
+        def quantise_fm(o, b, copy):
+            grouped = sbuf("grouped%d%d" % (o, b), [P, P, PACK], BF16)
+            copy(grouped[:], fm_rows[o][:, :, b::BLOCKS].rearrange("p t j -> p j t"))
+            fm_codes[o, b] = sbuf("fm_codes%d%d" % (o, b), [P, P], U32)
+            fm_planes[o, b] = sbuf("fm_planes%d%d" % (o, b), [P, P], U8)
+            nc.vector.quantize_mx(
+                out=fm_codes[o, b][:].bitcast(FP8X4),
+                scales=fm_planes[o, b][:],
+                in_=grouped[:].rearrange("p j t -> p (j t)"),
+            )
+
+        def product(o, n):
+            cols = slice(n * P, (n + 1) * P)
+            for b in range(BLOCKS):
+                nc.tensor.matmul_mx(
+                    out=y_bank[n][:, b * P : (b + 1) * P],
+                    lhsT=fm_codes[o, b][:].bitcast(FP8X4),
+                    lhsT_scale=fm_planes[o, b][:],
+                    rhs=picked_words[o][:, cols].bitcast(FP8X4),
+                    rhs_scale=picked_planes[4 * o :, cols],
+                    start=(o == 0 and b == 0),
+                    stop=(o == PASSES - 1 and b == BLOCKS - 1),
+                )
+
+        def turn_meas(n):
+            turned = bank("u%d" % n, "meas_bank%d" % n)
+            for b in range(BLOCKS):
+                nc.tensor.transpose(
+                    turned[:, b * P : (b + 1) * P], meas_rows[n // TILES][:, n % TILES, b::BLOCKS], ident[:]
+                )
+            meas_t[n] = sbuf("meas_t%d" % n, [P, R])
+            nc.scalar.copy(meas_t[n][:], turned[:, :R])
+            update_bank[n] = bank("u%d" % n, "update_bank%d" % n)
+            for b in range(BLOCKS):
+                cols = slice(b * P, (b + 1) * P)
+                transpose_into(update_bank[n][:, cols], meas_t[n][:, cols], b == 0, False)
+
+        prior_rep = sbuf("prior_rep", [P, G, RUN])
+        nc.gpsimd.tensor_scalar(
+            prior_rep[:], prior_row[:].unsqueeze(2).to_broadcast([P, G, RUN]), -0.5, 0.0, ALU.mult, ALU.add
+        )
+        prior_bank = bank("u3", "prior_bank")
+        nc.tensor.transpose(prior_bank[:, :P], prior_rep[:].rearrange("p g r -> p (g r)"), ident[:])
+        prior_t = sbuf("prior_t", [P, P])
+        nc.scalar.copy(prior_t[:], prior_bank[:, :P])
+
+        def misfit_runs(n):
+            return y_bank[n][:, R : R + G * PITCH].rearrange("p (g r) -> p g r", r=PITCH)
+
+        for n in range(HALVES * TILES):
+            y_bank[n] = bank("y%d" % n, "y_bank%d" % n)
+            nc.tensor.transpose(misfit_runs(n)[:, :, PITCH - RUN :], prior_t[:], ident[:])
+
+        gather_words(0, 0, S)
+        nc.vector.tensor_copy(picked_planes[:], planes[:].indirect(picks[:]))
+        for b in range(BLOCKS):
+            quantise_fm(0, b, nc.scalar.copy)
+        for n in range(4):
+            turn_meas(n)
+        for n in range(HALVES * TILES):
+            product(0, n)
+        quantise_fm(1, 0, nc.vector.tensor_copy)
+        quantise_fm(1, 1, nc.scalar.copy)
+
+        half_prec = sbuf("half_prec", [P, BLOCKS])
+        nc.gpsimd.tensor_scalar(half_prec[:], prec_col[:], 0.5, 0.0, ALU.mult, ALU.add)
+        gain_less_one = sbuf("gain_less_one", [P, BLOCKS])
+        nc.gpsimd.tensor_scalar(gain_less_one[:], gain_col[:], 1.0, -1.0, ALU.mult, ALU.add)
+
+        def track_tile(n):
+            gather_words(1, n * P, (n + 1) * P)
+            product(1, n)
+            if n >= 4:
+                turn_meas(n)
+            dd = sbuf("dd%d" % n, [P, R])
+            d2 = sbuf("d2%d" % n, [P, R])
+            step = sbuf("step%d" % n, [P, R])
+            nc.vector.tensor_tensor(dd[:], meas_t[n][:], y_bank[n][:, :R], ALU.subtract)
+            for b in range(BLOCKS):
+                cols = slice(b * P, (b + 1) * P)
+                nc.vector.scalar_tensor_tensor(
+                    d2[:, cols], dd[:, cols], half_prec[:, b : b + 1], dd[:, cols], ALU.mult, ALU.mult
+                )
+                transpose_into(misfit_runs(n)[:, :, :RUN], d2[:, cols], b == 0, b == BLOCKS - 1)
+            for b in range(BLOCKS):
+                cols = slice(b * P, (b + 1) * P)
+                nc.scalar.activation(step[:, cols], dd[:, cols], ACT.Copy, scale=gain_less_one[:, b : b + 1])
+                transpose_into(update_bank[n][:, cols], step[:, cols], False, b == BLOCKS - 1)
+
+            misfit = sbuf("misfit%d" % n, [P, G])
+            nc.vector.tensor_reduce(
+                misfit[:], misfit_runs(n), AXIS_X, ALU.add
+            )
+            least = sbuf("least%d" % n, [P, 1])
+            nc.vector.tensor_reduce(least[:], misfit[:], AXIS_X, ALU.min)
+            weights = sbuf("weights%d" % n, [P, G])
+            total = sbuf("total%d" % n, [P, 1])
+            nc.scalar.activation(weights[:], misfit[:], ACT.Exp, bias=least[:], scale=-1.0, accum_out=total[:])
+
+            updated = update_bank[n][:, :R].rearrange("p (b g j) -> p g j b", b=BLOCKS, g=G)
+            weighted = windows[n][:, :R].rearrange("p (g j b) -> p g j b", b=BLOCKS, g=G)
+            if n in ():
+                nc.vector.tensor_tensor(
+                    weighted,
+                    updated,
+                    weights[:].unsqueeze(2).unsqueeze(3).to_broadcast([P, G, RUN, BLOCKS]),
+                    ALU.mult,
+                )
+            else:
+                for g in range(G):
+                    nc.scalar.activation(weighted[:, g], updated[:, g], ACT.Copy, scale=weights[:, g : g + 1])
+            gathered = sbuf("gathered%d" % n, [P, R])
+            nc.vector.tensor_copy(gathered[:], windows[n][:].indirect(by_feature[:]))
+            summed = sbuf("summed%d" % n, [P, D])
+            view = gathered[:].rearrange("p (v g) -> p v g", g=G)
+            if n in ():
+                four = sbuf("four%d" % n, [P, D, 4])
+                two = sbuf("two%d" % n, [P, D, 2])
+                nc.gpsimd.tensor_tensor(four[:], view[:, :, 0:4], view[:, :, 4:8], ALU.add)
+                nc.gpsimd.tensor_tensor(two[:], four[:, :, 0:2], four[:, :, 2:4], ALU.add)
+                nc.gpsimd.tensor_tensor(summed[:], two[:, :, 0], two[:, :, 1], ALU.add)
+            else:
+                nc.vector.tensor_reduce(summed[:], view, AXIS_X, ALU.add)
+            inverse = sbuf("inverse%d" % n, [P, 1])
+            nc.vector.reciprocal(inverse[:], total[:])
+            result = sbuf("result%d" % n, [P, D])
+            nc.scalar.activation(result[:], summed[:], ACT.Copy, scale=inverse[:])
+            nc.sync.dma_start(out[n * P : (n + 1) * P, :], result[:])
+
+        for n in range(HALVES * TILES):
+            track_tile(n)

@@ -60,7 +60,7 @@ def tile_picked_yimm_mean_p_kernel(
         warm = sbuf("warm", [P, 1])
         warm_out = sbuf("warm_out", [P, 1])
 
-        nc.vector.memset(planes[:].bitcast(I32), 0)
+        nc.gpsimd.memset(planes[:].bitcast(I32), 0)
         nc.vector.memset(warm[:], 0.0)
         nc.scalar.activation(warm_out[:], warm[:], ACT.Exp)
         make_identity(nc, ident[:])
@@ -86,16 +86,16 @@ def tile_picked_yimm_mean_p_kernel(
                 )
 
         nc.sync.dma_start(picks[:], offs)
-        nc.sync.dma_start(prior_row[:], prior)
-        load_words(0)
-        load_planes()
-        load_fm(0)
         load_meas(0)
         load_meas(1)
+        load_planes()
+        load_fm(0)
+        nc.sync.dma_start(prior_row[:], prior)
+        load_words(0)
         load_fm(1)
+        load_words(1)
         nc.sync.dma_start(prec_col[:], prec[0, :].rearrange("(p b) -> p b", b=BLOCKS))
         nc.sync.dma_start(gain_col[:], gain[0, :].rearrange("(p b) -> p b", b=BLOCKS))
-        load_words(1)
         nc.sync.dma_start(by_feature[:], byf)
 
         picked_words = [sbuf("picked_words%d" % o, [P, S], U32) for o in range(PASSES)]
@@ -149,11 +149,12 @@ def tile_picked_yimm_mean_p_kernel(
                 cols = slice(b * P, (b + 1) * P)
                 transpose_into(update_bank[n][:, cols], meas_t[n][:, cols], b == 0, False)
 
+        for n in range(HALVES * TILES):
+            turn_meas(n)
+
         prior_rep = sbuf("prior_rep", [P, G, RUN])
-        nc.gpsimd.tensor_scalar(
-            prior_rep[:], prior_row[:].unsqueeze(2).to_broadcast([P, G, RUN]), -0.5, 0.0, ALU.mult, ALU.add
-        )
-        prior_bank = bank("u3", "prior_bank")
+        nc.scalar.activation(prior_rep[:], prior_row[:].unsqueeze(2).to_broadcast([P, G, RUN]), ACT.Copy, scale=-0.5)
+        prior_bank = bank("y3", "prior_bank")
         nc.tensor.transpose(prior_bank[:, :P], prior_rep[:].rearrange("p g r -> p (g r)"), ident[:])
         prior_t = sbuf("prior_t", [P, P])
         nc.scalar.copy(prior_t[:], prior_bank[:, :P])
@@ -165,27 +166,23 @@ def tile_picked_yimm_mean_p_kernel(
             y_bank[n] = bank("y%d" % n, "y_bank%d" % n)
             nc.tensor.transpose(misfit_runs(n)[:, :, PITCH - RUN :], prior_t[:], ident[:])
 
-        gather_words(0, 0, S)
         nc.vector.tensor_copy(picked_planes[:], planes[:].indirect(picks[:]))
-        for b in range(BLOCKS):
-            quantise_fm(0, b, nc.scalar.copy)
-        for n in range(4):
-            turn_meas(n)
+        gather_words(0, 0, S)
+        quantise_fm(0, 0, nc.vector.tensor_copy)
+        quantise_fm(0, 1, nc.scalar.copy)
         for n in range(HALVES * TILES):
             product(0, n)
         quantise_fm(1, 0, nc.vector.tensor_copy)
         quantise_fm(1, 1, nc.scalar.copy)
 
         half_prec = sbuf("half_prec", [P, BLOCKS])
-        nc.gpsimd.tensor_scalar(half_prec[:], prec_col[:], 0.5, 0.0, ALU.mult, ALU.add)
+        nc.scalar.activation(half_prec[:], prec_col[:], ACT.Copy, scale=0.5)
         gain_less_one = sbuf("gain_less_one", [P, BLOCKS])
-        nc.gpsimd.tensor_scalar(gain_less_one[:], gain_col[:], 1.0, -1.0, ALU.mult, ALU.add)
+        nc.scalar.activation(gain_less_one[:], gain_col[:], ACT.Copy, bias=-1.0)
 
         def track_tile(n):
             gather_words(1, n * P, (n + 1) * P)
             product(1, n)
-            if n >= 4:
-                turn_meas(n)
             dd = sbuf("dd%d" % n, [P, R])
             d2 = sbuf("d2%d" % n, [P, R])
             step = sbuf("step%d" % n, [P, R])

@@ -37,8 +37,8 @@ def tile_picked_yimm_mean_p_kernel(
         sb = ctx.enter_context(tc.tile_pool(name="sb", bufs=1))
         ps = ctx.enter_context(tc.psum_pool(name="ps", bufs=1))
 
-        def sbuf(name, shape, dtype=F32):
-            return sb.tile(shape, dtype, name=name, align_bytes=64)
+        def sbuf(name, shape, dtype=F32, tag=""):
+            return sb.tile(shape, dtype, name=name, tag=tag or name, align_bytes=64)
 
         def bank(tag, name):
             return ps.tile([P, 512], F32, name=name, tag=tag)
@@ -180,9 +180,16 @@ def tile_picked_yimm_mean_p_kernel(
         gain_less_one = sbuf("gain_less_one", [P, BLOCKS])
         nc.scalar.activation(gain_less_one[:], gain_col[:], ACT.Copy, bias=-1.0)
 
-        def track_tile(n):
-            gather_words(1, n * P, (n + 1) * P)
+        gather_words(1, 0, P)
+        product(1, 0)
+        gather_words(1, P, S)
+        for n in range(1, HALVES * TILES):
             product(1, n)
+
+        sums = sbuf("sums", [P, HALVES * TILES + 1, D])
+        totals = sbuf("totals", [P, HALVES * TILES])
+
+        def track_tile(n):
             dd = sbuf("dd%d" % n, [P, R])
             d2 = sbuf("d2%d" % n, [P, R])
             step = sbuf("step%d" % n, [P, R])
@@ -204,9 +211,8 @@ def tile_picked_yimm_mean_p_kernel(
             )
             least = sbuf("least%d" % n, [P, 1])
             nc.vector.tensor_reduce(least[:], misfit[:], AXIS_X, ALU.min)
-            weights = sbuf("weights%d" % n, [P, G])
-            total = sbuf("total%d" % n, [P, 1])
-            nc.scalar.activation(weights[:], misfit[:], ACT.Exp, bias=least[:], scale=-1.0, accum_out=total[:])
+            weights = sums[:, n, :G]
+            nc.scalar.activation(weights, misfit[:], ACT.Exp, bias=least[:], scale=-1.0, accum_out=totals[:, n : n + 1])
 
             updated = update_bank[n][:, :R].rearrange("p (b g j) -> p g j b", b=BLOCKS, g=G)
             weighted = windows[n][:, :R].rearrange("p (g j b) -> p g j b", b=BLOCKS, g=G)
@@ -214,7 +220,7 @@ def tile_picked_yimm_mean_p_kernel(
                 nc.vector.tensor_tensor(
                     weighted,
                     updated,
-                    weights[:].unsqueeze(2).unsqueeze(3).to_broadcast([P, G, RUN, BLOCKS]),
+                    weights.unsqueeze(2).unsqueeze(3).to_broadcast([P, G, RUN, BLOCKS]),
                     ALU.mult,
                 )
             else:
@@ -222,21 +228,21 @@ def tile_picked_yimm_mean_p_kernel(
                     nc.scalar.activation(weighted[:, g], updated[:, g], ACT.Copy, scale=weights[:, g : g + 1])
             gathered = sbuf("gathered%d" % n, [P, R])
             nc.vector.tensor_copy(gathered[:], windows[n][:].indirect(by_feature[:]))
-            summed = sbuf("summed%d" % n, [P, D])
-            view = gathered[:].rearrange("p (v g) -> p v g", g=G)
-            if n in ():
-                four = sbuf("four%d" % n, [P, D, 4])
-                two = sbuf("two%d" % n, [P, D, 2])
-                nc.gpsimd.tensor_tensor(four[:], view[:, :, 0:4], view[:, :, 4:8], ALU.add)
-                nc.gpsimd.tensor_tensor(two[:], four[:, :, 0:2], four[:, :, 2:4], ALU.add)
-                nc.gpsimd.tensor_tensor(summed[:], two[:, :, 0], two[:, :, 1], ALU.add)
-            else:
-                nc.vector.tensor_reduce(summed[:], view, AXIS_X, ALU.add)
-            inverse = sbuf("inverse%d" % n, [P, 1])
-            nc.vector.reciprocal(inverse[:], total[:])
-            result = sbuf("result%d" % n, [P, D])
-            nc.scalar.activation(result[:], summed[:], ACT.Copy, scale=inverse[:])
-            nc.sync.dma_start(out[n * P : (n + 1) * P, :], result[:])
+            return gathered
 
-        for n in range(HALVES * TILES):
-            track_tile(n)
+        def sum_modes(n, gathered):
+            nc.vector.tensor_reduce(sums[:, n + 1, :], gathered[:].rearrange("p (v g) -> p v g", g=G), AXIS_X, ALU.add)
+
+        pending = track_tile(0)
+        for n in range(1, HALVES * TILES):
+            following = track_tile(n)
+            sum_modes(n - 1, pending)
+            pending = following
+        inverse = sbuf("inverse", [P, HALVES * TILES])
+        nc.vector.reciprocal(inverse[:], totals[:])
+        sum_modes(HALVES * TILES - 1, pending)
+        result = sbuf("result", [P, HALVES * TILES, D])
+        nc.vector.tensor_tensor(
+            result[:], sums[:, 1:, :], inverse[:].unsqueeze(2).to_broadcast([P, HALVES * TILES, D]), ALU.mult
+        )
+        nc.sync.dma_start(out.rearrange("(i p) v -> p i v", p=P), result[:])

from contextlib import ExitStack

import concourse.mybir as mybir
from concourse.masks import make_identity

K, T, S, R, G, D = 1024, 1024, 512, 256, 8, 32
FLOPS = 2 * K * S * R

F32 = mybir.dt.float32
BF16 = mybir.dt.bfloat16
I32 = mybir.dt.int32
U32 = mybir.dt.uint32
U16 = mybir.dt.uint16
U8 = mybir.dt.uint8
FP8X4 = mybir.dt.float8_e4m3fn_x4
ALU = mybir.AluOpType
ACT = mybir.ActivationFunctionType
AXIS_X = mybir.AxisListType.X

P = 128
PACK = 4
PASSES = K // (P * PACK)
BLOCKS = R // P
HALVES = 2
HALF = S // HALVES
TILES = HALF // P
RUN = D // BLOCKS
WINDOW = 352
PITCH = RUN + 2


def tile_picked_yimm_mean_p_kernel(
    tc, x_words, x_scales, fm, meas, prec, prior, gain, offs, byf, out
):
    nc = tc.nc
    with ExitStack() as ctx:
        sb = ctx.enter_context(tc.tile_pool(name="sb", bufs=1))
        ps = ctx.enter_context(tc.psum_pool(name="ps", bufs=1))

        def sbuf(name, shape, dtype=F32, tag=""):
            return sb.tile(shape, dtype, name=name, tag=tag or name, align_bytes=64)

        def bank(tag, name):
            return ps.tile([P, 512], F32, name=name, tag=tag)

        def transpose_into(dst, src, first, last):
            nc.tensor.matmul(dst, src, ident[:], start=first, stop=last, is_transpose=True)

        picks = sb.tile([P, S // 16], U16, name="picks")
        by_feature = sb.tile([P, R // 16], U16, name="by_feature")
        words = [sbuf("words%d" % o, [P, T], I32) for o in range(PASSES)]
        planes = sbuf("planes", [P, T], U8)
        fm_rows = [sbuf("fm_rows%d" % o, [P, PACK, R]) for o in range(PASSES)]
        meas_rows = [sbuf("meas_rows%d" % h, [P, TILES, R]) for h in range(HALVES)]
        prec_col = sbuf("prec_col", [P, BLOCKS])
        gain_col = sbuf("gain_col", [P, BLOCKS])
        prior_row = sbuf("prior_row", [P, G])
        windows = [sbuf("window%d" % n, [P, WINDOW]) for n in range(HALVES * TILES)]
        ident = sbuf("ident", [P, P])
        warm = sbuf("warm", [P, 1])
        warm_out = sbuf("warm_out", [P, 1])

        nc.gpsimd.memset(planes[:].bitcast(I32), 0)
        nc.vector.memset(warm[:], 0.0)
        nc.scalar.activation(warm_out[:], warm[:], ACT.Exp)
        make_identity(nc, ident[:])
        for window in windows:
            nc.vector.memset(window[:, R:], 0.0)

        def load_words(o):
            nc.sync.dma_start(words[o][:], x_words[o].rearrange("p n t -> p (n t)").bitcast(I32))

        def load_fm(o):
            rows = fm[o * P * PACK : (o + 1) * P * PACK, :]
            nc.sync.dma_start(fm_rows[o][:], rows.rearrange("(p t) e -> p t e", t=PACK))

        def load_meas(h):
            rows = meas[h * HALF : (h + 1) * HALF, :]
            nc.sync.dma_start(meas_rows[h][:], rows.rearrange("(i p) e -> p i e", p=P))

        def load_planes():
            for q in range(4):
                nc.sync.dma_start(
                    planes[32 * q : 32 * q + 4 * PASSES, :].bitcast(I32),
                    x_scales[:, 4 * q : 4 * q + 4, :].bitcast(I32),
                )

        nc.sync.dma_start(picks[:], offs)
        load_meas(0)
        load_meas(1)
        load_planes()
        load_fm(0)
        nc.sync.dma_start(prior_row[:], prior)
        load_words(0)
        load_fm(1)
        load_words(1)
        nc.sync.dma_start(prec_col[:], prec[0, :].rearrange("(p b) -> p b", b=BLOCKS))
        nc.sync.dma_start(gain_col[:], gain[0, :].rearrange("(p b) -> p b", b=BLOCKS))
        nc.sync.dma_start(by_feature[:], byf)

        picked_words = [sbuf("picked_words%d" % o, [P, S], U32) for o in range(PASSES)]
        picked_planes = sbuf("picked_planes", [P, S], U8)
        fm_codes = {}
        fm_planes = {}
        y_bank = {}
        meas_t = {}
        update_bank = {}
        misfit_bank = {}

        def gather_words(o, lo, hi):
            nc.vector.tensor_copy(
                picked_words[o][:, lo:hi], words[o][:].bitcast(U32).indirect(picks[:, lo // 16 : hi // 16])
            )

        def quantise_fm(o, b, copy):
            grouped = sbuf("grouped%d%d" % (o, b), [P, P, PACK], BF16)
            copy(grouped[:], fm_rows[o][:, :, b::BLOCKS].rearrange("p t j -> p j t"))
            fm_codes[o, b] = sbuf("fm_codes%d%d" % (o, b), [P, P], U32)
            fm_planes[o, b] = sbuf("fm_planes%d%d" % (o, b), [P, P], U8)
            nc.vector.quantize_mx(
                out=fm_codes[o, b][:].bitcast(FP8X4),
                scales=fm_planes[o, b][:],
                in_=grouped[:].rearrange("p j t -> p (j t)"),
            )

        def product(o, n):
            cols = slice(n * P, (n + 1) * P)
            for b in range(BLOCKS):
                nc.tensor.matmul_mx(
                    out=y_bank[n][:, b * P : (b + 1) * P],
                    lhsT=fm_codes[o, b][:].bitcast(FP8X4),
                    lhsT_scale=fm_planes[o, b][:],
                    rhs=picked_words[o][:, cols].bitcast(FP8X4),
                    rhs_scale=picked_planes[4 * o :, cols],
                    start=(o == 0 and b == 0),
                    stop=(o == PASSES - 1 and b == BLOCKS - 1),
                )

        def turn_meas(n):
            turned = bank("u%d" % n, "meas_bank%d" % n)
            for b in range(BLOCKS):
                nc.tensor.transpose(
                    turned[:, b * P : (b + 1) * P], meas_rows[n // TILES][:, n % TILES, b::BLOCKS], ident[:]
                )
            meas_t[n] = sbuf("meas_t%d" % n, [P, R])
            nc.scalar.copy(meas_t[n][:], turned[:, :R])
            update_bank[n] = bank("u%d" % n, "update_bank%d" % n)
            for b in range(BLOCKS):
                cols = slice(b * P, (b + 1) * P)
                transpose_into(update_bank[n][:, cols], meas_t[n][:, cols], b == 0, False)

        for n in range(HALVES * TILES):
            turn_meas(n)

        prior_rep = sbuf("prior_rep", [P, G, RUN])
        nc.scalar.activation(prior_rep[:], prior_row[:].unsqueeze(2).to_broadcast([P, G, RUN]), ACT.Copy, scale=-0.5)
        prior_bank = bank("y3", "prior_bank")
        nc.tensor.transpose(prior_bank[:, :P], prior_rep[:].rearrange("p g r -> p (g r)"), ident[:])
        prior_t = sbuf("prior_t", [P, P])
        nc.scalar.copy(prior_t[:], prior_bank[:, :P])

        def misfit_runs(n):
            return y_bank[n][:, R : R + G * PITCH].rearrange("p (g r) -> p g r", r=PITCH)

        for n in range(HALVES * TILES):
            y_bank[n] = bank("y%d" % n, "y_bank%d" % n)
            nc.tensor.transpose(misfit_runs(n)[:, :, PITCH - RUN :], prior_t[:], ident[:])

        nc.vector.tensor_copy(picked_planes[:], planes[:].indirect(picks[:]))
        gather_words(0, 0, S)
        quantise_fm(0, 0, nc.vector.tensor_copy)
        quantise_fm(0, 1, nc.scalar.copy)
        for n in range(HALVES * TILES):
            product(0, n)
        quantise_fm(1, 0, nc.vector.tensor_copy)
        quantise_fm(1, 1, nc.scalar.copy)

        half_prec = sbuf("half_prec", [P, BLOCKS])
        nc.scalar.activation(half_prec[:], prec_col[:], ACT.Copy, scale=0.5)
        gain_less_one = sbuf("gain_less_one", [P, BLOCKS])
        nc.scalar.activation(gain_less_one[:], gain_col[:], ACT.Copy, bias=-1.0)

        gather_words(1, 0, P)
        product(1, 0)
        gather_words(1, P, S)
        for n in range(1, HALVES * TILES):
            product(1, n)

        sums = sbuf("sums", [P, HALVES * TILES + 1, D])
        totals = sbuf("totals", [P, HALVES * TILES])

        def track_tile(n):
            dd = sbuf("dd%d" % n, [P, R])
            d2 = sbuf("d2%d" % n, [P, R])
            step = sbuf("step%d" % n, [P, R])
            nc.vector.tensor_tensor(dd[:], meas_t[n][:], y_bank[n][:, :R], ALU.subtract)
            for b in range(BLOCKS):
                cols = slice(b * P, (b + 1) * P)
                nc.vector.scalar_tensor_tensor(
                    d2[:, cols], dd[:, cols], half_prec[:, b : b + 1], dd[:, cols], ALU.mult, ALU.mult
                )
                transpose_into(misfit_runs(n)[:, :, :RUN], d2[:, cols], b == 0, b == BLOCKS - 1)
            for b in range(BLOCKS):
                cols = slice(b * P, (b + 1) * P)
                nc.scalar.activation(step[:, cols], dd[:, cols], ACT.Copy, scale=gain_less_one[:, b : b + 1])
                transpose_into(update_bank[n][:, cols], step[:, cols], False, b == BLOCKS - 1)

            misfit = sbuf("misfit%d" % n, [P, G])
            nc.vector.tensor_reduce(
                misfit[:], misfit_runs(n), AXIS_X, ALU.add
            )
            least = sbuf("least%d" % n, [P, 1])
            nc.vector.tensor_reduce(least[:], misfit[:], AXIS_X, ALU.min)
            weights = sums[:, n, :G]
            nc.scalar.activation(weights, misfit[:], ACT.Exp, bias=least[:], scale=-1.0, accum_out=totals[:, n : n + 1])

            updated = update_bank[n][:, :R].rearrange("p (b g j) -> p g j b", b=BLOCKS, g=G)
            weighted = windows[n][:, :R].rearrange("p (g j b) -> p g j b", b=BLOCKS, g=G)
            if n in ():
                nc.vector.tensor_tensor(
                    weighted,
                    updated,
                    weights.unsqueeze(2).unsqueeze(3).to_broadcast([P, G, RUN, BLOCKS]),
                    ALU.mult,
                )
            else:
                for g in range(G):
                    nc.scalar.activation(weighted[:, g], updated[:, g], ACT.Copy, scale=weights[:, g : g + 1])
            gathered = sbuf("gathered%d" % n, [P, R])
            nc.vector.tensor_copy(gathered[:], windows[n][:].indirect(by_feature[:]))
            return gathered

        def sum_modes(n, gathered):
            nc.vector.tensor_reduce(sums[:, n + 1, :], gathered[:].rearrange("p (v g) -> p v g", g=G), AXIS_X, ALU.add)

        pending = track_tile(0)
        for n in range(1, HALVES * TILES):
            following = track_tile(n)
            sum_modes(n - 1, pending)
            pending = following
        inverse = sbuf("inverse", [P, HALVES * TILES])
        nc.vector.reciprocal(inverse[:], totals[:])
        sum_modes(HALVES * TILES - 1, pending)
        result = sbuf("result", [P, HALVES * TILES, D])
        nc.vector.tensor_tensor(
            result[:], sums[:, 1:, :], inverse[:].unsqueeze(2).to_broadcast([P, HALVES * TILES, D]), ALU.mult
        )
        nc.sync.dma_start(out.rearrange("(i p) v -> p i v", p=P), result[:])
